import numpy as np
import ml_dtypes


def mxq(x, axis, fmt="e4m3"):
    dtype, down = {"e4m3": (ml_dtypes.float8_e4m3fn, 7), "e5m2": (ml_dtypes.float8_e5m2, 14)}[fmt]
    v = np.moveaxis(np.asarray(x, np.float32).astype(ml_dtypes.bfloat16).astype(np.float64), axis, -1)
    blocks = v.reshape(v.shape[:-1] + (-1, 32))
    amax = np.abs(blocks).max(-1, keepdims=True)
    byte = np.maximum(np.where(amax > 0, np.frexp(amax)[1] - 1 + 127, 0) - down, 1)
    scale = np.exp2(byte - 127.0)
    codes = (blocks / scale).astype(np.float32).astype(dtype).astype(np.float64)
    return np.moveaxis((codes * scale).reshape(v.shape), -1, axis)


WIDE = False


def mx_kscale(k):
    if not WIDE:
        return np.ones(k)
    levels = np.array([10, -10, 5, -5, 0])
    if k % 512:
        return np.exp2(np.random.permutation(np.resize(levels, k // 32))).repeat(32)
    a = np.empty((k // 512, 16))
    for p in range(k // 512):
        a[p, :8] = np.random.permutation(np.resize(levels, 8))
        for g in range(8):
            far = levels[np.abs(levels - a[p, g]) >= 10]
            a[p, g + 8] = far[np.random.randint(len(far))]
    return np.exp2(a.ravel()).repeat(32)


BF16 = ml_dtypes.bfloat16


def bf(x):
    return np.asarray(x, np.float32).astype(BF16)


def f64(x):
    return np.asarray(x).astype(np.float64)


E2M1 = np.array([0.0, 0.5, 1.0, 1.5, 2.0, 3.0, 4.0, 6.0, -0.0, -0.5, -1.0, -1.5, -2.0, -3.0, -4.0, -6.0])


def pack_weight(w, fmt):
    k, n = w.shape
    w = f64(bf(w)).reshape(k // 32, 32, n)
    amax = np.abs(w).max(1)
    if fmt == "e4m3":
        byte = np.frexp(amax)[1] - 1 + 127 - 7
    else:
        mant, ex = np.frexp(amax / 6.0)
        byte = np.where(mant > 0.5, ex, ex - 1) + 127
    byte = np.clip(np.where(amax > 0, byte, 1), 1, 254)
    scaled = (w * np.exp2(127.0 - byte)[:, None, :]).reshape(k, n).astype(np.float32)
    by_word = np.ascontiguousarray(scaled.reshape(k // 512, 128, 4, n).transpose(0, 1, 3, 2))
    if fmt == "e4m3":
        words = by_word.astype(ml_dtypes.float8_e4m3fn).view(np.uint8)
    else:
        c = by_word.astype(ml_dtypes.float4_e2m1fn).view(np.uint8) & 0xF
        words = c[..., 0::2] | (c[..., 1::2] << 4)
    return np.ascontiguousarray(words), np.ascontiguousarray(byte.astype(np.uint8).reshape(k // 512, 16, n))


def unpack_weight(words, scales, fmt):
    g, p, n, _ = words.shape
    if fmt == "e4m3":
        vals = np.ascontiguousarray(words).view(ml_dtypes.float8_e4m3fn).astype(np.float64)
    else:
        nib = np.empty((g, p, n, 4), np.uint8)
        nib[..., 0::2] = words & 0xF
        nib[..., 1::2] = words >> 4
        vals = E2M1[nib]
    vals = vals * np.repeat(np.exp2(scales.astype(np.float64) - 127.0), 8, axis=1)[..., None]
    return vals.transpose(0, 1, 3, 2).reshape(g * 512, n)
def pack4(w):
    words, scales = pack_weight(w, "e2m1")
    return words.reshape(words.shape[0], 128, -1), scales


def unpack4(words, scales):
    return unpack_weight(words.reshape(words.shape[0], 128, -1, 2), scales, "e2m1")


def planes(Y):
    n, m = Y.shape
    b = f64(bf(Y)).reshape(n // 32, 32, m)
    amax = np.abs(b).max(1)
    byte = np.clip(np.where(amax > 0, np.frexp(amax)[1] - 1 + 127 - 7, 1), 1, 254)
    codes = (b * np.exp2(127.0 - byte)[:, None, :]).reshape(n, m).astype(np.float32).astype(ml_dtypes.float8_e4m3fn).view(np.uint8)
    words = codes.reshape(n // 512, 128, 4, m).transpose(0, 1, 3, 2)
    return np.ascontiguousarray(words), np.ascontiguousarray(byte.astype(np.uint8).reshape(n // 512, 16, m))


G, A, B = 4, 1024, 512

def setup_inputs():
    r = np.random.randn
    s = mx_kscale(G * A).reshape(G, A, 1)
    t = mx_kscale(G * B).reshape(G, B)
    snk = r(G, A, A) / np.sqrt(A) * s
    src = r(G, B, B) / np.sqrt(B) * np.exp(0.8 * r(G, 1, B)) / t[:, :, None]
    snk_words, snk_scales = pack4(snk.reshape(G * A, A))
    src_words, src_scales = pack4(src.reshape(G * B, B))
    return {
        "tau": bf(r(G, A, B) / s),
        "back": bf(r(G, A, B)),
        "src_weight": bf(np.exp(0.3 * r(G, B)) * t),
        "snk_weight": bf(np.exp(0.3 * r(G, A))),
        "snk_words": snk_words, "snk_scales": snk_scales,
        "src_words": src_words, "src_scales": src_scales,
    }

def reference(tau, back, src_weight, snk_weight, snk_words, snk_scales, src_words, src_scales):
    E = unpack4(snk_words, snk_scales).reshape(G, A, A)
    S = unpack4(src_words, src_scales).reshape(G, B, B)
    h = (E.swapaxes(1, 2) @ mxq(f64(tau), 1, "e4m3")) * f64(src_weight)[:, None, :]
    chain = mxq(h, 2, "e4m3") @ S
    y = chain * f64(back) * f64(snk_weight)[:, :, None]
    Y = y.reshape(G * A, B).T
    words, scales = planes(Y)
    return y, words, scales

@@ -1,0 +1,306 @@
+from contextlib import ExitStack
+
+import concourse.mybir as mybir
+from concourse.masks import make_identity
+
+G, A, B = 4, 1024, 512
+FLOPS = 2 * G * (A * A * B + A * B * B)
+
+F32 = mybir.dt.float32
+BF16 = mybir.dt.bfloat16
+I32 = mybir.dt.int32
+U32 = mybir.dt.uint32
+U8 = mybir.dt.uint8
+FP8X4 = mybir.dt.float8_e4m3fn_x4
+FP4X4 = mybir.dt.float4_e2m1fn_x4
+MULT = mybir.AluOpType.mult
+
+P = 128
+PACK = 4
+KP = P * PACK
+HALVES = 2 * G
+WROWS = HALVES + G
+
+
+def tile_distilled_meson_correlator_k7_kernel(
+    tc, tau, back, src_weight, snk_weight, snk_words, snk_scales, src_words, src_scales, out_0, out_1, out_2
+):
+    nc = tc.nc
+    with ExitStack() as ctx:
+        keep = ctx.enter_context(tc.tile_pool(name="keep", bufs=1))
+        work = ctx.enter_context(tc.tile_pool(name="work", bufs=2))
+        psum = ctx.enter_context(tc.psum_pool(name="psum", bufs=1))
+        ctx.enter_context(tc.manual_schedule())
+
+        tau_raw, back_sb, e_words, s_words = {}, {}, {}, {}
+        tau_il, tau_codes, tau_scales = {}, {}, {}
+        h_bank, h_il, h_codes, h_scales = {}, {}, {}, {}
+        chain_bank, y32, y16, yt_bank, yt_il = {}, {}, {}, {}, {}
+
+        ident = keep.tile([P, P], F32, name="ident")
+        w_rows16 = keep.tile([P, KP], BF16, name="w_rows16")
+        w_rows32 = keep.tile([P, KP], F32, name="w_rows32")
+        w_cols = keep.tile([P, WROWS, PACK], F32, name="w_cols")
+        e_scales_first = keep.tile([P, 2, A], U8, name="e_scales_first", align_bytes=64)
+        e_scales_rest = keep.tile([P, 2 * (G - 1), A], U8, name="e_scales_rest", align_bytes=64)
+        s_scales = keep.tile([P, G, B], U8, name="s_scales", align_bytes=64)
+        y_scales = keep.tile([P, A], U8, name="y_scales", align_bytes=64)
+
+        def load_tau(c, g):
+            tau_raw[c, g] = keep.tile([P, PACK, B], BF16, name="tau_raw_%d_%d" % (c, g))
+            nc.sync.dma_start(
+                out=tau_raw[c, g][:], in_=tau[c, g * KP : (g + 1) * KP, :].rearrange("(p j) b -> p j b", j=PACK)
+            )
+
+        def load_back(u):
+            c, h = divmod(u, 2)
+            back_sb[u] = keep.tile([P, PACK, B], BF16, name="back_%d" % u)
+            nc.sync.dma_start(
+                out=back_sb[u][:], in_=back[c, h * KP : (h + 1) * KP, :].rearrange("(p n) j -> p n j", n=PACK)
+            )
+
+        def load_e(c):
+            e_words[c] = keep.tile([P, 2, 2 * A], U8, name="e_words_%d" % c, align_bytes=64)
+            nc.sync.dma_start(
+                out=e_words[c][:].bitcast(I32),
+                in_=snk_words[2 * c : 2 * c + 2].rearrange("g p n -> p g n").bitcast(I32),
+            )
+
+        def load_s(c0, c1):
+            words = keep.tile([P, c1 - c0, 2 * B], U8, name="s_words_%d" % c0, align_bytes=64)
+            nc.sync.dma_start(
+                out=words[:].bitcast(I32), in_=src_words[c0:c1].rearrange("g p n -> p g n").bitcast(I32)
+            )
+            for c in range(c0, c1):
+                s_words[c] = words[:, c - c0, :]
+
+        def load_scale_rows(plane, rows):
+            for q in range(4):
+                nc.sync.dma_start(
+                    out=plane[32 * q : 32 * q + 4, :, :].bitcast(I32),
+                    in_=rows[:, 4 * q : 4 * q + 4, :].rearrange("g r n -> r g n").bitcast(I32),
+                )
+
+        def interleave_tau(copy, c, g, m0, m1):
+            if (c, g) not in tau_il:
+                tau_il[c, g] = work.tile([P, PACK * B], BF16, name="tau_il", bufs=3, align_bytes=64)
+            dst = tau_il[c, g][:].rearrange("p (t a b j) -> p a t b j", t=PACK, b=2, j=PACK)
+            src = tau_raw[c, g][:].rearrange("p j (a b t) -> p a t b j", b=2, t=PACK)
+            copy(out=dst[:, m0 // 2 : m1 // 2], in_=src[:, m0 // 2 : m1 // 2])
+
+        def quantize_tau(c, g):
+            tau_codes[c, g] = work.tile([P, B], U32, name="tau_codes", bufs=4, align_bytes=64)
+            tau_scales[c, g] = work.tile([P, B], U8, name="tau_scales", bufs=4, align_bytes=64)
+            nc.vector.quantize_mx(
+                out=tau_codes[c, g][:].bitcast(FP8X4), scales=tau_scales[c, g][:], in_=tau_il[c, g][:]
+            )
+
+        def stage1(u, k):
+            c, h = divmod(u, 2)
+            bank = psum.tile([P, PACK, P], F32, name="h_bank", bufs=3)
+            h_bank[u, k] = bank
+            i0 = h * KP + k * P
+            for t in range(PACK):
+                for g in range(2):
+                    plane = e_scales_first[:, g, :] if c == 0 else e_scales_rest[:, 2 * (c - 1) + g, :]
+                    nc.tensor.matmul_mx(
+                        out=bank[:, t, :],
+                        lhsT=tau_codes[c, g][:, t * P : (t + 1) * P].bitcast(FP8X4),
+                        lhsT_scale=tau_scales[c, g][:, t * P : (t + 1) * P],
+                        rhs=e_words[c][:, g, 2 * i0 : 2 * (i0 + P)].bitcast(FP4X4),
+                        rhs_scale=plane[:, i0 : i0 + P],
+                        start=(g == 0),
+                        stop=(g == 1),
+                    )
+
+        def weigh_h(u, k):
+            if k == 0:
+                h_il[u] = work.tile([P, PACK, P, PACK], BF16, name="h_il", align_bytes=64)
+            row = HALVES + u // 2
+            nc.vector.tensor_tensor(
+                out=h_il[u][:, :, 32 * k : 32 * (k + 1), :],
+                in0=h_bank[u, k][:].rearrange("p t (r n) -> p n r t", n=PACK),
+                in1=w_cols[:, row : row + 1, :].unsqueeze(1).broadcast_to([P, PACK, 32, PACK]),
+                op=MULT,
+            )
+
+        def quantize_h(u):
+            h_codes[u] = work.tile([P, KP], U32, name="h_codes", align_bytes=64)
+            h_scales[u] = work.tile([P, KP], U8, name="h_scales", align_bytes=64)
+            nc.vector.quantize_mx(
+                out=h_codes[u][:].bitcast(FP8X4),
+                scales=h_scales[u][:],
+                in_=h_il[u][:].rearrange("p n r t -> p (n r t)"),
+            )
+
+        def stage2(u, n):
+            c = u // 2
+            bank = psum.tile([P, B], F32, name="chain_bank", bufs=3)
+            chain_bank[u, n] = bank
+            nc.tensor.matmul_mx(
+                out=bank[:],
+                lhsT=h_codes[u][:, n * P : (n + 1) * P].bitcast(FP8X4),
+                lhsT_scale=h_scales[u][:, n * P : (n + 1) * P],
+                rhs=s_words[c].bitcast(FP4X4),
+                rhs_scale=s_scales[:, c, :],
+                start=True,
+                stop=True,
+            )
+
+        def weigh_y(u, n):
+            if n == 0:
+                y32[u] = work.tile([P, PACK, B], F32, name="y32", bufs=5)
+            nc.vector.scalar_tensor_tensor(
+                out=y32[u][:, n, :],
+                in0=chain_bank[u, n][:],
+                scalar=w_cols[:, u, n : n + 1],
+                in1=back_sb[u][:, n, :],
+                op0=MULT,
+                op1=MULT,
+            )
+
+        def round_y(u, n):
+            y16[u, n] = work.tile([P, B], BF16, name="y16", bufs=6)
+            nc.scalar.copy(out=y16[u, n][:], in_=y32[u][:, n, :])
+
+        def turn_y(u, pair):
+            bank = psum.tile([P, 2, 2, P], F32, name="yt_bank", bufs=2)
+            yt_bank[u, pair] = bank
+            for d in range(2):
+                words = y16[u, 2 * pair + d][:].bitcast(F32)
+                for e in range(2):
+                    nc.tensor.transpose(bank[:, d, e, :], words[:, e : B // 2 : 2], ident[:])
+
+        def gather_yt(u, pair):
+            if pair == 0:
+                yt_il[u] = work.tile([P, PACK * KP], BF16, name="yt_il", align_bytes=64)
+            dst = yt_il[u][:].bitcast(F32).rearrange("p (r n e) -> p r n e", n=PACK, e=2)
+            nc.scalar.copy(
+                out=dst[:, :, 2 * pair : 2 * pair + 2, :], in_=yt_bank[u, pair][:].rearrange("p d e r -> p r d e")
+            )
+
+        def quantize_and_store_yt(u):
+            c, h = divmod(u, 2)
+            codes = work.tile([P, KP], U32, name="y_codes", bufs=5, align_bytes=64)
+            nc.vector.quantize_mx(
+                out=codes[:].bitcast(FP8X4), scales=y_scales[4 * c : P, h * KP : (h + 1) * KP], in_=yt_il[u][:]
+            )
+            nc.sync.dma_start(
+                out=out_1[0, :, u * KP : (u + 1) * KP, :].rearrange("p m t -> p (m t)").bitcast(I32),
+                in_=codes[:].bitcast(I32),
+            )
+
+        def store_y(u, n0, n1):
+            c, h = divmod(u, 2)
+            rows = out_0[c, h * KP : (h + 1) * KP, :].rearrange("(p n) j -> p n j", n=PACK)
+            nc.sync.dma_start(out=rows[:, n0:n1, :], in_=y32[u][:, n0:n1, :])
+
+        nc.vector.memset(e_scales_first[:].bitcast(I32), 0)
+        nc.vector.memset(s_scales[:].bitcast(I32), 0)
+        nc.vector.memset(e_scales_rest[:].bitcast(I32), 0)
+        make_identity(nc, ident[:])
+        nc.gpsimd.memset(w_rows32[:], 0.0)
+
+        nc.scalar.dma_start(out=w_rows16[0:HALVES, :], in_=snk_weight.rearrange("c (h x) -> (c h) x", h=2))
+        nc.scalar.dma_start(out=w_rows16[HALVES:WROWS, :], in_=src_weight)
+        load_tau(0, 0)
+        load_tau(0, 1)
+        load_e(0)
+        load_scale_rows(e_scales_first, snk_scales[0:2])
+        load_tau(1, 0)
+        load_s(0, 1)
+        load_scale_rows(s_scales, src_scales)
+        load_back(0)
+        load_tau(1, 1)
+        load_scale_rows(e_scales_rest, snk_scales[2 : 2 * G])
+        load_e(1)
+        load_back(1)
+        load_tau(2, 0)
+        load_s(1, G)
+        load_back(2)
+        load_tau(2, 1)
+        load_e(2)
+        load_back(3)
+        load_tau(3, 0)
+        load_tau(3, 1)
+        load_back(4)
+        load_e(3)
+        for u in range(5, HALVES):
+            load_back(u)
+
+        nc.scalar.copy(out=w_rows32[0:WROWS, :], in_=w_rows16[0:WROWS, :])
+        w_bank = psum.tile([P, 2, 2, P], F32, name="yt_bank", bufs=2)
+        w_bank_cols = w_bank[:].rearrange("p d e r -> p (d e) r")
+        for t in range(PACK):
+            nc.tensor.transpose(w_bank_cols[:, t, :], w_rows32[:, t:KP:PACK], ident[:])
+
+        interleave_tau(nc.vector.tensor_copy, 0, 0, 0, 96)
+        interleave_tau(nc.scalar.copy, 0, 0, 96, P)
+        nc.scalar.copy(out=w_cols[:], in_=w_bank_cols[:, :, 0:WROWS].rearrange("p t r -> p r t"))
+        interleave_tau(nc.vector.tensor_copy, 0, 1, 0, 64)
+        interleave_tau(nc.scalar.copy, 0, 1, 64, P)
+        quantize_tau(0, 0)
+        quantize_tau(0, 1)
+        stage1(0, 0)
+        stage1(0, 1)
+        interleave_tau(nc.scalar.copy, 1, 0, 0, P)
+
+        for s in range(-1, HALVES):
+            has_h = s + 1 < HALVES
+            has_y = s >= 0
+            il_c, il_g = divmod(s + 4, 2)
+            q_c, q_g = divmod(s + 3, 2)
+
+            def piece(k):
+                if il_c < G:
+                    interleave_tau(nc.scalar.copy, il_c, il_g, 32 * k, 32 * (k + 1))
+
+            if has_y:
+                stage2(s, 0)
+                stage2(s, 1)
+            if s >= 1:
+                turn_y(s - 1, 1)
+            if has_h:
+                stage1(s + 1, 2)
+            if has_y:
+                stage2(s, 2)
+            piece(0)
+            if s >= 1:
+                gather_yt(s - 1, 1)
+            for k in range(PACK):
+                if has_h:
+                    weigh_h(s + 1, k)
+                    if k == 0:
+                        stage1(s + 1, 3)
+                if has_y:
+                    weigh_y(s, k)
+                    if k == 0:
+                        stage2(s, 3)
+                    round_y(s, k)
+                    if s == HALVES - 1 and k % 2 == 1:
+                        store_y(s, k - 1, k + 1)
+                if k == 0 and q_c < G:
+                    quantize_tau(q_c, q_g)
+                if k == 1 and has_y:
+                    turn_y(s, 0)
+                if k == 2 and has_y:
+                    gather_yt(s, 0)
+                if k in (1, 2) and s + 2 < HALVES:
+                    stage1(s + 2, k - 1)
+                if k < 3:
+                    piece(k + 1)
+            if has_y and s < HALVES - 1:
+                store_y(s, 0, PACK)
+            if has_h:
+                quantize_h(s + 1)
+            if s >= 1:
+                quantize_and_store_yt(s - 1)
+
+        turn_y(HALVES - 1, 1)
+        gather_yt(HALVES - 1, 1)
+        quantize_and_store_yt(HALVES - 1)
+        for q in range(4):
+            nc.sync.dma_start(
+                out=out_2[0, 4 * q : 4 * q + 4, :].rearrange("r (c m) -> c r m", c=G).bitcast(I32),
+                in_=y_scales[32 * q : 32 * q + 16, :].bitcast(I32),
+            )

@@ -19,7 +19,8 @@ P = 128
 PACK = 4
 KP = P * PACK
 HALVES = 2 * G
-WROWS = HALVES + G
+SNK_ROWS = PACK * HALVES
+WROWS = SNK_ROWS + G
 
 
 def tile_distilled_meson_correlator_k7_kernel(
@@ -40,6 +41,7 @@ def tile_distilled_meson_correlator_k7_kernel(
         ident = keep.tile([P, P], F32, name="ident")
         w_rows16 = keep.tile([P, KP], BF16, name="w_rows16")
         w_rows32 = keep.tile([P, KP], F32, name="w_rows32")
+        zero = keep.tile([P, 1], F32, name="zero")
         w_cols = keep.tile([P, WROWS, PACK], F32, name="w_cols")
         e_scales_first = keep.tile([P, 2, A], U8, name="e_scales_first", align_bytes=64)
         e_scales_rest = keep.tile([P, 2 * (G - 1), A], U8, name="e_scales_rest", align_bytes=64)
@@ -56,7 +58,7 @@ def tile_distilled_meson_correlator_k7_kernel(
             c, h = divmod(u, 2)
             back_sb[u] = keep.tile([P, PACK, B], BF16, name="back_%d" % u)
             nc.sync.dma_start(
-                out=back_sb[u][:], in_=back[c, h * KP : (h + 1) * KP, :].rearrange("(p n) j -> p n j", n=PACK)
+                out=back_sb[u][:], in_=back[c, h * KP : (h + 1) * KP, :].rearrange("(n p) j -> p n j", n=PACK)
             )
 
         def load_e(c):
@@ -115,12 +117,12 @@ def tile_distilled_meson_correlator_k7_kernel(
 
         def weigh_h(u, k):
             if k == 0:
-                h_il[u] = work.tile([P, PACK, P, PACK], BF16, name="h_il", align_bytes=64)
-            row = HALVES + u // 2
+                h_il[u] = work.tile([P, PACK, P * PACK], BF16, name="h_il", align_bytes=64)
+            row = SNK_ROWS + u // 2
             nc.vector.tensor_tensor(
-                out=h_il[u][:, :, 32 * k : 32 * (k + 1), :],
-                in0=h_bank[u, k][:].rearrange("p t (r n) -> p n r t", n=PACK),
-                in1=w_cols[:, row : row + 1, :].unsqueeze(1).broadcast_to([P, PACK, 32, PACK]),
+                out=h_il[u][:, k, :].rearrange("p (a b t) -> p a t b", b=2, t=PACK),
+                in0=h_bank[u, k][:].rearrange("p t (a b) -> p a t b", b=2),
+                in1=w_cols[:, row : row + 1, :].unsqueeze(3).broadcast_to([P, P // 2, PACK, 2]),
                 op=MULT,
             )
 
@@ -130,12 +132,12 @@ def tile_distilled_meson_correlator_k7_kernel(
             nc.vector.quantize_mx(
                 out=h_codes[u][:].bitcast(FP8X4),
                 scales=h_scales[u][:],
-                in_=h_il[u][:].rearrange("p n r t -> p (n r t)"),
+                in_=h_il[u][:].rearrange("p n x -> p (n x)"),
             )
 
-        def stage2(u, n):
+        def stage2(u, n, tag="chain_bank"):
             c = u // 2
-            bank = psum.tile([P, B], F32, name="chain_bank", bufs=3)
+            bank = psum.tile([P, B], F32, name=tag, bufs=3)
             chain_bank[u, n] = bank
             nc.tensor.matmul_mx(
                 out=bank[:],
@@ -153,56 +155,63 @@ def tile_distilled_meson_correlator_k7_kernel(
             nc.vector.scalar_tensor_tensor(
                 out=y32[u][:, n, :],
                 in0=chain_bank[u, n][:],
-                scalar=w_cols[:, u, n : n + 1],
+                scalar=w_cols[:, PACK * u + n, 0:1],
                 in1=back_sb[u][:, n, :],
                 op0=MULT,
                 op1=MULT,
             )
 
-        def round_y(u, n):
-            y16[u, n] = work.tile([P, B], BF16, name="y16", bufs=6)
-            nc.scalar.copy(out=y16[u, n][:], in_=y32[u][:, n, :])
+        def round_y(copy, u, n):
+            y16[u, n] = work.tile([P, B], BF16, name="y16", bufs=8)
+            copy(
+                out=y16[u, n][:].rearrange("p (e m z) -> p e m z", e=2, z=2),
+                in_=y32[u][:, n, :].rearrange("p (m e z) -> p e m z", e=2, z=2),
+            )
 
-        def turn_y(u, pair):
-            bank = psum.tile([P, 2, 2, P], F32, name="yt_bank", bufs=2)
+        def turn_y(u, pair, tag, bufs):
+            bank = psum.tile([P, 2, 2, P], F32, name=tag, bufs=bufs)
             yt_bank[u, pair] = bank
             for d in range(2):
                 words = y16[u, 2 * pair + d][:].bitcast(F32)
                 for e in range(2):
-                    nc.tensor.transpose(bank[:, d, e, :], words[:, e : B // 2 : 2], ident[:])
+                    nc.tensor.transpose(bank[:, d, e, :], words[:, e * P : (e + 1) * P], ident[:])
 
-        def gather_yt(u, pair):
+        def gather_yt(copy, u, pair):
             if pair == 0:
                 yt_il[u] = work.tile([P, PACK * KP], BF16, name="yt_il", align_bytes=64)
-            dst = yt_il[u][:].bitcast(F32).rearrange("p (r n e) -> p r n e", n=PACK, e=2)
-            nc.scalar.copy(
-                out=dst[:, :, 2 * pair : 2 * pair + 2, :], in_=yt_bank[u, pair][:].rearrange("p d e r -> p r d e")
+            dst = yt_il[u][:].bitcast(F32).rearrange("p (n a b e) -> p n a e b", n=PACK, b=2, e=2)
+            copy(
+                out=dst[:, 2 * pair : 2 * pair + 2],
+                in_=yt_bank[u, pair][:].rearrange("p d e (a b) -> p d a e b", b=2),
             )
 
-        def quantize_and_store_yt(u):
+        def quantize_and_store_yt(u, m0, m1):
             c, h = divmod(u, 2)
             codes = work.tile([P, KP], U32, name="y_codes", bufs=5, align_bytes=64)
             nc.vector.quantize_mx(
-                out=codes[:].bitcast(FP8X4), scales=y_scales[4 * c : P, h * KP : (h + 1) * KP], in_=yt_il[u][:]
+                out=codes[:, m0:m1].bitcast(FP8X4),
+                scales=y_scales[4 * c : P, h * KP + m0 : h * KP + m1],
+                in_=yt_il[u][:, PACK * m0 : PACK * m1],
             )
             nc.sync.dma_start(
-                out=out_1[0, :, u * KP : (u + 1) * KP, :].rearrange("p m t -> p (m t)").bitcast(I32),
-                in_=codes[:].bitcast(I32),
+                out=out_1[0, :, u * KP + m0 : u * KP + m1, :].rearrange("p m t -> p (m t)").bitcast(I32),
+                in_=codes[:, m0:m1].bitcast(I32),
             )
 
         def store_y(u, n0, n1):
             c, h = divmod(u, 2)
-            rows = out_0[c, h * KP : (h + 1) * KP, :].rearrange("(p n) j -> p n j", n=PACK)
+            rows = out_0[c, h * KP : (h + 1) * KP, :].rearrange("(n p) j -> p n j", n=PACK)
             nc.sync.dma_start(out=rows[:, n0:n1, :], in_=y32[u][:, n0:n1, :])
 
+        nc.vector.memset(zero[:], 0.0)
         nc.vector.memset(e_scales_first[:].bitcast(I32), 0)
         nc.vector.memset(s_scales[:].bitcast(I32), 0)
         nc.vector.memset(e_scales_rest[:].bitcast(I32), 0)
         make_identity(nc, ident[:])
-        nc.gpsimd.memset(w_rows32[:], 0.0)
 
-        nc.scalar.dma_start(out=w_rows16[0:HALVES, :], in_=snk_weight.rearrange("c (h x) -> (c h) x", h=2))
-        nc.scalar.dma_start(out=w_rows16[HALVES:WROWS, :], in_=src_weight)
+        nc.scalar.dma_start(out=w_rows16[0:SNK_ROWS, 0:P], in_=snk_weight.rearrange("c (n x) -> (c n) x", x=P))
+        nc.scalar.dma_start(out=w_rows16[SNK_ROWS:WROWS, :], in_=src_weight)
+        nc.scalar.copy(out=w_rows32[:], in_=zero[:].to_broadcast([P, KP]))
         load_tau(0, 0)
         load_tau(0, 1)
         load_e(0)
@@ -228,7 +237,8 @@ def tile_distilled_meson_correlator_k7_kernel(
         for u in range(5, HALVES):
             load_back(u)
 
-        nc.scalar.copy(out=w_rows32[0:WROWS, :], in_=w_rows16[0:WROWS, :])
+        nc.scalar.copy(out=w_rows32[SNK_ROWS:WROWS, :], in_=w_rows16[SNK_ROWS:WROWS, :])
+        nc.scalar.copy(out=w_rows32[0:SNK_ROWS, 0:KP:PACK], in_=w_rows16[0:SNK_ROWS, 0:P])
         w_bank = psum.tile([P, 2, 2, P], F32, name="yt_bank", bufs=2)
         w_bank_cols = w_bank[:].rearrange("p d e r -> p (d e) r")
         for t in range(PACK):
@@ -243,62 +253,72 @@ def tile_distilled_meson_correlator_k7_kernel(
         quantize_tau(0, 1)
         stage1(0, 0)
         stage1(0, 1)
-        interleave_tau(nc.scalar.copy, 1, 0, 0, P)
 
-        for s in range(-1, HALVES):
-            has_h = s + 1 < HALVES
+        last = HALVES - 1
+        for s in range(-1, last):
             has_y = s >= 0
-            il_c, il_g = divmod(s + 4, 2)
-            q_c, q_g = divmod(s + 3, 2)
-
-            def piece(k):
-                if il_c < G:
-                    interleave_tau(nc.scalar.copy, il_c, il_g, 32 * k, 32 * (k + 1))
-
+            next_c, next_g = divmod(s + 3, 2)
             if has_y:
                 stage2(s, 0)
                 stage2(s, 1)
-            if s >= 1:
-                turn_y(s - 1, 1)
-            if has_h:
-                stage1(s + 1, 2)
+            stage1(s + 1, 2)
             if has_y:
                 stage2(s, 2)
-            piece(0)
             if s >= 1:
-                gather_yt(s - 1, 1)
+                turn_y(s - 1, 0, "yt_bank", 2)
+                turn_y(s - 1, 1, "yt_bank", 2)
+            if next_c < G:
+                interleave_tau(nc.scalar.copy, next_c, next_g, 0, P)
             for k in range(PACK):
-                if has_h:
-                    weigh_h(s + 1, k)
-                    if k == 0:
-                        stage1(s + 1, 3)
+                weigh_h(s + 1, k)
+                if k == 0:
+                    stage1(s + 1, 3)
                 if has_y:
                     weigh_y(s, k)
                     if k == 0:
                         stage2(s, 3)
-                    round_y(s, k)
-                    if s == HALVES - 1 and k % 2 == 1:
-                        store_y(s, k - 1, k + 1)
-                if k == 0 and q_c < G:
-                    quantize_tau(q_c, q_g)
-                if k == 1 and has_y:
-                    turn_y(s, 0)
-                if k == 2 and has_y:
-                    gather_yt(s, 0)
-                if k in (1, 2) and s + 2 < HALVES:
-                    stage1(s + 2, k - 1)
-                if k < 3:
-                    piece(k + 1)
-            if has_y and s < HALVES - 1:
+                    round_y(nc.scalar.copy, s, k)
+                if k == 0 and s >= 1:
+                    gather_yt(nc.scalar.copy, s - 1, 0)
+                    gather_yt(nc.scalar.copy, s - 1, 1)
+                if k == 2:
+                    if next_c < G and next_g == 1:
+                        quantize_tau(next_c, next_g)
+                    if s + 2 < HALVES:
+                        stage1(s + 2, 0)
+                        stage1(s + 2, 1)
+            if has_y:
                 store_y(s, 0, PACK)
-            if has_h:
-                quantize_h(s + 1)
+            quantize_h(s + 1)
+            if next_c < G and next_g == 0:
+                quantize_tau(next_c, next_g)
             if s >= 1:
-                quantize_and_store_yt(s - 1)
+                quantize_and_store_yt(s - 1, 0, KP)
 
-        turn_y(HALVES - 1, 1)
-        gather_yt(HALVES - 1, 1)
-        quantize_and_store_yt(HALVES - 1)
+        for n in range(3):
+            stage2(last, n)
+        stage2(last, 3, "h_bank")
+        turn_y(last - 1, 0, "yt_bank", 2)
+        turn_y(last - 1, 1, "yt_bank", 2)
+        weigh_y(last, 0)
+        round_y(nc.scalar.copy, last, 0)
+        weigh_y(last, 1)
+        round_y(nc.scalar.copy, last, 1)
+        store_y(last, 0, 2)
+        turn_y(last, 0, "h_bank", 3)
+        gather_yt(nc.scalar.copy, last - 1, 0)
+        gather_yt(nc.scalar.copy, last - 1, 1)
+        weigh_y(last, 2)
+        weigh_y(last, 3)
+        store_y(last, 2, 4)
+        round_y(nc.vector.tensor_copy, last, 2)
+        round_y(nc.vector.tensor_copy, last, 3)
+        turn_y(last, 1, "h_bank", 3)
+        quantize_and_store_yt(last - 1, 0, KP)
+        gather_yt(nc.scalar.copy, last, 0)
+        gather_yt(nc.scalar.copy, last, 1)
+        quantize_and_store_yt(last, 0, KP // 2)
+        quantize_and_store_yt(last, KP // 2, KP)
         for q in range(4):
             nc.sync.dma_start(
                 out=out_2[0, 4 * q : 4 * q + 4, :].rearrange("r (c m) -> c r m", c=G).bitcast(I32),

@@ -14,6 +14,8 @@ U8 = mybir.dt.uint8
 FP8X4 = mybir.dt.float8_e4m3fn_x4
 FP4X4 = mybir.dt.float4_e2m1fn_x4
 MULT = mybir.AluOpType.mult
+ADD = mybir.AluOpType.add
+COPY = mybir.ActivationFunctionType.Copy
 
 P = 128
 PACK = 4
@@ -115,9 +117,25 @@ def tile_distilled_meson_correlator_k7_kernel(
                         stop=(g == 1),
                     )
 
-        def weigh_h(u, k):
-            if k == 0:
+        def open_h(u):
+            if u not in h_il:
                 h_il[u] = work.tile([P, PACK, P * PACK], BF16, name="h_il", align_bytes=64)
+
+        def weigh_h_on_scalar(u, k):
+            open_h(u)
+            row = SNK_ROWS + u // 2
+            slots = work.tile([P, PACK, P], BF16, name="h_slots")
+            for t in range(PACK):
+                nc.scalar.activation(
+                    out=slots[:, t, :], in_=h_bank[u, k][:, t, :], func=COPY, scale=w_cols[:, row, t : t + 1]
+                )
+            nc.scalar.copy(
+                out=h_il[u][:, k, :].rearrange("p (a b t) -> p a t b", b=4, t=PACK),
+                in_=slots[:].rearrange("p t (a b) -> p a t b", b=4),
+            )
+
+        def weigh_h(u, k):
+            open_h(u)
             row = SNK_ROWS + u // 2
             nc.vector.tensor_tensor(
                 out=h_il[u][:, k, :].rearrange("p (a b t) -> p a t b", b=2, t=PACK),
@@ -161,20 +179,26 @@ def tile_distilled_meson_correlator_k7_kernel(
                 op1=MULT,
             )
 
-        def round_y(copy, u, n):
-            y16[u, n] = work.tile([P, B], BF16, name="y16", bufs=8)
-            copy(
-                out=y16[u, n][:].rearrange("p (e m z) -> p e m z", e=2, z=2),
-                in_=y32[u][:, n, :].rearrange("p (m e z) -> p e m z", e=2, z=2),
-            )
+        def gpsimd_copy(out, in_):
+            nc.gpsimd.tensor_scalar(out=out, in0=in_, scalar1=1.0, scalar2=-0.0, op0=MULT, op1=ADD)
+
+        def round_y(copy, u, pair, d0, d1, host=None):
+            if (u, pair) not in y16:
+                if host is None:
+                    host = work.tile([P, 2 * B], BF16, name="y16", bufs=3)
+                y16[u, pair] = host[:, 0 : 2 * B]
+            dst = y16[u, pair].rearrange("p (e d m z) -> p e d m z", e=2, d=2, z=2)
+            src = y32[u][:, 2 * pair : 2 * pair + 2, :].rearrange("p d (m e z) -> p e d m z", e=2, z=2)
+            copy(out=dst[:, :, d0:d1], in_=src[:, :, d0:d1])
 
         def turn_y(u, pair, tag, bufs):
             bank = psum.tile([P, 2, 2, P], F32, name=tag, bufs=bufs)
             yt_bank[u, pair] = bank
+            words = y16[u, pair].bitcast(F32)
             for d in range(2):
-                words = y16[u, 2 * pair + d][:].bitcast(F32)
                 for e in range(2):
-                    nc.tensor.transpose(bank[:, d, e, :], words[:, e * P : (e + 1) * P], ident[:])
+                    x0 = (2 * e + d) * P
+                    nc.tensor.transpose(bank[:, d, e, :], words[:, x0 : x0 + P], ident[:])
 
         def gather_yt(copy, u, pair):
             if pair == 0:
@@ -209,8 +233,8 @@ def tile_distilled_meson_correlator_k7_kernel(
         nc.vector.memset(e_scales_rest[:].bitcast(I32), 0)
         make_identity(nc, ident[:])
 
-        nc.scalar.dma_start(out=w_rows16[0:SNK_ROWS, 0:P], in_=snk_weight.rearrange("c (n x) -> (c n) x", x=P))
-        nc.scalar.dma_start(out=w_rows16[SNK_ROWS:WROWS, :], in_=src_weight)
+        nc.sync.dma_start(out=w_rows16[0:SNK_ROWS, 0:P], in_=snk_weight.rearrange("c (n x) -> (c n) x", x=P))
+        nc.sync.dma_start(out=w_rows16[SNK_ROWS:WROWS, :], in_=src_weight)
         nc.scalar.copy(out=w_rows32[:], in_=zero[:].to_broadcast([P, KP]))
         load_tau(0, 0)
         load_tau(0, 1)
@@ -237,8 +261,8 @@ def tile_distilled_meson_correlator_k7_kernel(
         for u in range(5, HALVES):
             load_back(u)
 
-        nc.scalar.copy(out=w_rows32[SNK_ROWS:WROWS, :], in_=w_rows16[SNK_ROWS:WROWS, :])
-        nc.scalar.copy(out=w_rows32[0:SNK_ROWS, 0:KP:PACK], in_=w_rows16[0:SNK_ROWS, 0:P])
+        nc.vector.tensor_copy(out=w_rows32[SNK_ROWS:WROWS, :], in_=w_rows16[SNK_ROWS:WROWS, :])
+        nc.vector.tensor_copy(out=w_rows32[0:SNK_ROWS, 0:KP:PACK], in_=w_rows16[0:SNK_ROWS, 0:P])
         w_bank = psum.tile([P, 2, 2, P], F32, name="yt_bank", bufs=2)
         w_bank_cols = w_bank[:].rearrange("p d e r -> p (d e) r")
         for t in range(PACK):
@@ -251,59 +275,65 @@ def tile_distilled_meson_correlator_k7_kernel(
         interleave_tau(nc.scalar.copy, 0, 1, 64, P)
         quantize_tau(0, 0)
         quantize_tau(0, 1)
-        stage1(0, 0)
-        stage1(0, 1)
+        for k in range(3):
+            stage1(0, k)
+        interleave_tau(nc.scalar.copy, 1, 0, 0, P)
+        for k in range(PACK):
+            weigh_h(0, k)
+            stage1(*divmod(k + 3, PACK))
+        quantize_h(0)
+        quantize_tau(1, 0)
 
         last = HALVES - 1
-        for s in range(-1, last):
-            has_y = s >= 0
+        for s in range(last):
             next_c, next_g = divmod(s + 3, 2)
-            if has_y:
-                stage2(s, 0)
-                stage2(s, 1)
-            stage1(s + 1, 2)
-            if has_y:
-                stage2(s, 2)
+            early = next_c < G
+            ahead = s + 2 < HALVES
+            for n in range(3):
+                stage2(s, n)
+            if s >= 1:
+                round_y(gpsimd_copy, s - 1, 1, 0, 2, yt_il.get(s - 2))
+            if early:
+                interleave_tau(nc.scalar.copy, next_c, next_g, 0, P)
+            else:
+                weigh_h_on_scalar(s + 1, 2)
+            weigh_h(s + 1, 0)
+            stage1(s + 1, 3)
+            weigh_y(s, 0)
             if s >= 1:
                 turn_y(s - 1, 0, "yt_bank", 2)
                 turn_y(s - 1, 1, "yt_bank", 2)
-            if next_c < G:
-                interleave_tau(nc.scalar.copy, next_c, next_g, 0, P)
-            for k in range(PACK):
-                weigh_h(s + 1, k)
-                if k == 0:
-                    stage1(s + 1, 3)
-                if has_y:
-                    weigh_y(s, k)
-                    if k == 0:
-                        stage2(s, 3)
-                    round_y(nc.scalar.copy, s, k)
-                if k == 0 and s >= 1:
-                    gather_yt(nc.scalar.copy, s - 1, 0)
-                    gather_yt(nc.scalar.copy, s - 1, 1)
-                if k == 2:
-                    if next_c < G and next_g == 1:
-                        quantize_tau(next_c, next_g)
-                    if s + 2 < HALVES:
-                        stage1(s + 2, 0)
-                        stage1(s + 2, 1)
-            if has_y:
-                store_y(s, 0, PACK)
-            quantize_h(s + 1)
-            if next_c < G and next_g == 0:
+            stage2(s, 3)
+            weigh_y(s, 1)
+            round_y(gpsimd_copy, s, 0, 0, 2)
+            weigh_h_on_scalar(s + 1, 3)
+            weigh_h(s + 1, 1)
+            weigh_y(s, 2)
+            if early:
                 quantize_tau(next_c, next_g)
+                weigh_h(s + 1, 2)
+            weigh_y(s, 3)
+            if ahead:
+                for k in range(3):
+                    stage1(s + 2, k)
+            if s >= 1:
+                gather_yt(nc.scalar.copy, s - 1, 0)
+                gather_yt(nc.scalar.copy, s - 1, 1)
+            store_y(s, 0, PACK)
+            quantize_h(s + 1)
             if s >= 1:
                 quantize_and_store_yt(s - 1, 0, KP)
 
         for n in range(3):
             stage2(last, n)
         stage2(last, 3, "h_bank")
+        round_y(gpsimd_copy, last - 1, 1, 0, 2, yt_il[last - 2])
         turn_y(last - 1, 0, "yt_bank", 2)
         turn_y(last - 1, 1, "yt_bank", 2)
         weigh_y(last, 0)
-        round_y(nc.scalar.copy, last, 0)
+        round_y(nc.scalar.copy, last, 0, 0, 1)
         weigh_y(last, 1)
-        round_y(nc.scalar.copy, last, 1)
+        round_y(nc.scalar.copy, last, 0, 1, 2)
         store_y(last, 0, 2)
         turn_y(last, 0, "h_bank", 3)
         gather_yt(nc.scalar.copy, last - 1, 0)
@@ -311,8 +341,8 @@ def tile_distilled_meson_correlator_k7_kernel(
         weigh_y(last, 2)
         weigh_y(last, 3)
         store_y(last, 2, 4)
-        round_y(nc.vector.tensor_copy, last, 2)
-        round_y(nc.vector.tensor_copy, last, 3)
+        round_y(nc.vector.tensor_copy, last, 1, 0, 1)
+        round_y(nc.vector.tensor_copy, last, 1, 1, 2)
         turn_y(last, 1, "h_bank", 3)
         quantize_and_store_yt(last - 1, 0, KP)
         gather_yt(nc.scalar.copy, last, 0)

@@ -21,8 +21,9 @@ P = 128
 PACK = 4
 KP = P * PACK
 HALVES = 2 * G
-SNK_ROWS = PACK * HALVES
-WROWS = SNK_ROWS + G
+SNK_ROWS = 2 * HALVES
+SRC_ROW0 = 32
+WROWS = SRC_ROW0 + G
 
 
 def tile_distilled_meson_correlator_k7_kernel(
@@ -60,7 +61,8 @@ def tile_distilled_meson_correlator_k7_kernel(
             c, h = divmod(u, 2)
             back_sb[u] = keep.tile([P, PACK, B], BF16, name="back_%d" % u)
             nc.sync.dma_start(
-                out=back_sb[u][:], in_=back[c, h * KP : (h + 1) * KP, :].rearrange("(n p) j -> p n j", n=PACK)
+                out=back_sb[u][:].rearrange("p (d e) j -> p d (e j)", e=2),
+                in_=back[c, h * KP : (h + 1) * KP, :].rearrange("(d p e) j -> p d (e j)", d=2, e=2),
             )
 
         def load_e(c):
@@ -79,10 +81,10 @@ def tile_distilled_meson_correlator_k7_kernel(
                 s_words[c] = words[:, c - c0, :]
 
         def load_scale_rows(plane, rows):
-            for q in range(4):
+            for r in range(4):
                 nc.sync.dma_start(
-                    out=plane[32 * q : 32 * q + 4, :, :].bitcast(I32),
-                    in_=rows[:, 4 * q : 4 * q + 4, :].rearrange("g r n -> r g n").bitcast(I32),
+                    out=plane[r:P:32, :, :].bitcast(I32),
+                    in_=rows[:, r:16:4, :].rearrange("g q n -> q g n").bitcast(I32),
                 )
 
         def interleave_tau(copy, c, g, m0, m1):
@@ -117,30 +119,33 @@ def tile_distilled_meson_correlator_k7_kernel(
                         stop=(g == 1),
                     )
 
-        def open_h(u):
+        def h_window(u, k):
             if u not in h_il:
-                h_il[u] = work.tile([P, PACK, P * PACK], BF16, name="h_il", align_bytes=64)
+                h_il[u] = work.tile([P, PACK, P, PACK], BF16, name="h_il", align_bytes=64)
+            d, r0 = k // 2, 64 * (k % 2)
+            return h_il[u][:, 2 * d : 2 * d + 2, r0 : r0 + 64, :]
 
         def weigh_h_on_scalar(u, k):
-            open_h(u)
-            row = SNK_ROWS + u // 2
-            slots = work.tile([P, PACK, P], BF16, name="h_slots")
+            row = SRC_ROW0 + u // 2
+            slots = work.tile([P, PACK, 2, 64], BF16, name="h_slots")
             for t in range(PACK):
                 nc.scalar.activation(
-                    out=slots[:, t, :], in_=h_bank[u, k][:, t, :], func=COPY, scale=w_cols[:, row, t : t + 1]
+                    out=slots[:, t, :, :],
+                    in_=h_bank[u, k][:, t, :].rearrange("p (r e) -> p e r", e=2),
+                    func=COPY,
+                    scale=w_cols[:, row, t : t + 1],
                 )
             nc.scalar.copy(
-                out=h_il[u][:, k, :].rearrange("p (a b t) -> p a t b", b=4, t=PACK),
-                in_=slots[:].rearrange("p t (a b) -> p a t b", b=4),
+                out=h_window(u, k).rearrange("p e (a b) t -> p e a t b", b=4),
+                in_=slots[:].rearrange("p t e (a b) -> p e a t b", b=4),
             )
 
         def weigh_h(u, k):
-            open_h(u)
-            row = SNK_ROWS + u // 2
+            row = SRC_ROW0 + u // 2
             nc.vector.tensor_tensor(
-                out=h_il[u][:, k, :].rearrange("p (a b t) -> p a t b", b=2, t=PACK),
-                in0=h_bank[u, k][:].rearrange("p t (a b) -> p a t b", b=2),
-                in1=w_cols[:, row : row + 1, :].unsqueeze(3).broadcast_to([P, P // 2, PACK, 2]),
+                out=h_window(u, k).rearrange("p e r t -> p r e t"),
+                in0=h_bank[u, k][:].rearrange("p t (r e) -> p r e t", e=2),
+                in1=w_cols[:, row : row + 1, :].unsqueeze(1).broadcast_to([P, 64, 2, PACK]),
                 op=MULT,
             )
 
@@ -150,7 +155,7 @@ def tile_distilled_meson_correlator_k7_kernel(
             nc.vector.quantize_mx(
                 out=h_codes[u][:].bitcast(FP8X4),
                 scales=h_scales[u][:],
-                in_=h_il[u][:].rearrange("p n x -> p (n x)"),
+                in_=h_il[u][:].rearrange("p n r t -> p (n r t)"),
             )
 
         def stage2(u, n, tag="chain_bank"):
@@ -173,7 +178,7 @@ def tile_distilled_meson_correlator_k7_kernel(
             nc.vector.scalar_tensor_tensor(
                 out=y32[u][:, n, :],
                 in0=chain_bank[u, n][:],
-                scalar=w_cols[:, PACK * u + n, 0:1],
+                scalar=w_cols[:, 2 * u + n // 2, n % 2 : n % 2 + 1],
                 in1=back_sb[u][:, n, :],
                 op0=MULT,
                 op1=MULT,
@@ -203,11 +208,8 @@ def tile_distilled_meson_correlator_k7_kernel(
         def gather_yt(copy, u, pair):
             if pair == 0:
                 yt_il[u] = work.tile([P, PACK * KP], BF16, name="yt_il", align_bytes=64)
-            dst = yt_il[u][:].bitcast(F32).rearrange("p (n a b e) -> p n a e b", n=PACK, b=2, e=2)
-            copy(
-                out=dst[:, 2 * pair : 2 * pair + 2],
-                in_=yt_bank[u, pair][:].rearrange("p d e (a b) -> p d a e b", b=2),
-            )
+            dst = yt_il[u][:].bitcast(F32).rearrange("p (d a b x) -> p d a x b", d=2, b=2, x=PACK)
+            copy(out=dst[:, pair], in_=yt_bank[u, pair][:].rearrange("p d e (a b) -> p a (d e) b", b=2))
 
         def quantize_and_store_yt(u, m0, m1):
             c, h = divmod(u, 2)
@@ -222,10 +224,12 @@ def tile_distilled_meson_correlator_k7_kernel(
                 in_=codes[:, m0:m1].bitcast(I32),
             )
 
-        def store_y(u, n0, n1):
+        def store_y(u, d0, d1):
             c, h = divmod(u, 2)
-            rows = out_0[c, h * KP : (h + 1) * KP, :].rearrange("(n p) j -> p n j", n=PACK)
-            nc.sync.dma_start(out=rows[:, n0:n1, :], in_=y32[u][:, n0:n1, :])
+            rows = out_0[c, h * KP : (h + 1) * KP, :].rearrange("(d p e) j -> p d (e j)", d=2, e=2)
+            nc.sync.dma_start(
+                out=rows[:, d0:d1, :], in_=y32[u][:].rearrange("p (d e) j -> p d (e j)", e=2)[:, d0:d1, :]
+            )
 
         nc.vector.memset(zero[:], 0.0)
         nc.vector.memset(e_scales_first[:].bitcast(I32), 0)
@@ -233,25 +237,25 @@ def tile_distilled_meson_correlator_k7_kernel(
         nc.vector.memset(e_scales_rest[:].bitcast(I32), 0)
         make_identity(nc, ident[:])
 
-        nc.sync.dma_start(out=w_rows16[0:SNK_ROWS, 0:P], in_=snk_weight.rearrange("c (n x) -> (c n) x", x=P))
-        nc.sync.dma_start(out=w_rows16[SNK_ROWS:WROWS, :], in_=src_weight)
+        nc.sync.dma_start(out=w_rows16[0:SNK_ROWS, 0 : 2 * P], in_=snk_weight.rearrange("c (n x) -> (c n) x", x=2 * P))
+        nc.sync.dma_start(out=w_rows16[SRC_ROW0:WROWS, :], in_=src_weight)
         nc.scalar.copy(out=w_rows32[:], in_=zero[:].to_broadcast([P, KP]))
         load_tau(0, 0)
         load_tau(0, 1)
         load_e(0)
         load_scale_rows(e_scales_first, snk_scales[0:2])
+        load_scale_rows(s_scales, src_scales)
         load_tau(1, 0)
         load_s(0, 1)
-        load_scale_rows(s_scales, src_scales)
         load_back(0)
         load_tau(1, 1)
         load_scale_rows(e_scales_rest, snk_scales[2 : 2 * G])
         load_e(1)
-        load_back(1)
         load_tau(2, 0)
+        load_back(1)
+        load_tau(2, 1)
         load_s(1, G)
         load_back(2)
-        load_tau(2, 1)
         load_e(2)
         load_back(3)
         load_tau(3, 0)
@@ -261,8 +265,11 @@ def tile_distilled_meson_correlator_k7_kernel(
         for u in range(5, HALVES):
             load_back(u)
 
-        nc.vector.tensor_copy(out=w_rows32[SNK_ROWS:WROWS, :], in_=w_rows16[SNK_ROWS:WROWS, :])
-        nc.vector.tensor_copy(out=w_rows32[0:SNK_ROWS, 0:KP:PACK], in_=w_rows16[0:SNK_ROWS, 0:P])
+        nc.vector.tensor_copy(out=w_rows32[SRC_ROW0:WROWS, :], in_=w_rows16[SRC_ROW0:WROWS, :])
+        nc.vector.tensor_copy(
+            out=w_rows32[0:SNK_ROWS, :].rearrange("p (x t) -> p x t", t=PACK)[:, :, 0:2],
+            in_=w_rows16[0:SNK_ROWS, 0 : 2 * P].rearrange("p (x e) -> p x e", e=2),
+        )
         w_bank = psum.tile([P, 2, 2, P], F32, name="yt_bank", bufs=2)
         w_bank_cols = w_bank[:].rearrange("p d e r -> p (d e) r")
         for t in range(PACK):
@@ -283,19 +290,18 @@ def tile_distilled_meson_correlator_k7_kernel(
             stage1(*divmod(k + 3, PACK))
         quantize_h(0)
         quantize_tau(1, 0)
+        interleave_tau(nc.scalar.copy, 1, 1, 0, P)
 
         last = HALVES - 1
         for s in range(last):
-            next_c, next_g = divmod(s + 3, 2)
-            early = next_c < G
-            ahead = s + 2 < HALVES
+            ready = divmod(s + 3, 2)
+            coming = divmod(s + 4, 2)
+            scalar_is_free = coming[0] >= G
             for n in range(3):
                 stage2(s, n)
             if s >= 1:
                 round_y(gpsimd_copy, s - 1, 1, 0, 2, yt_il.get(s - 2))
-            if early:
-                interleave_tau(nc.scalar.copy, next_c, next_g, 0, P)
-            else:
+            if scalar_is_free:
                 weigh_h_on_scalar(s + 1, 2)
             weigh_h(s + 1, 0)
             stage1(s + 1, 3)
@@ -305,21 +311,24 @@ def tile_distilled_meson_correlator_k7_kernel(
                 turn_y(s - 1, 1, "yt_bank", 2)
             stage2(s, 3)
             weigh_y(s, 1)
-            round_y(gpsimd_copy, s, 0, 0, 2)
+            if ready[0] < G:
+                quantize_tau(*ready)
+            round_y(gpsimd_copy, s, 0, 0, 2, tau_il.get(ready))
             weigh_h_on_scalar(s + 1, 3)
             weigh_h(s + 1, 1)
             weigh_y(s, 2)
-            if early:
-                quantize_tau(next_c, next_g)
+            if not scalar_is_free:
                 weigh_h(s + 1, 2)
             weigh_y(s, 3)
-            if ahead:
+            if s + 2 < HALVES:
                 for k in range(3):
                     stage1(s + 2, k)
             if s >= 1:
                 gather_yt(nc.scalar.copy, s - 1, 0)
                 gather_yt(nc.scalar.copy, s - 1, 1)
-            store_y(s, 0, PACK)
+            if coming[0] < G:
+                interleave_tau(nc.scalar.copy, coming[0], coming[1], 0, P)
+            store_y(s, 0, 2)
             quantize_h(s + 1)
             if s >= 1:
                 quantize_and_store_yt(s - 1, 0, KP)
@@ -334,13 +343,13 @@ def tile_distilled_meson_correlator_k7_kernel(
         round_y(nc.scalar.copy, last, 0, 0, 1)
         weigh_y(last, 1)
         round_y(nc.scalar.copy, last, 0, 1, 2)
-        store_y(last, 0, 2)
+        store_y(last, 0, 1)
         turn_y(last, 0, "h_bank", 3)
         gather_yt(nc.scalar.copy, last - 1, 0)
         gather_yt(nc.scalar.copy, last - 1, 1)
         weigh_y(last, 2)
         weigh_y(last, 3)
-        store_y(last, 2, 4)
+        store_y(last, 1, 2)
         round_y(nc.vector.tensor_copy, last, 1, 0, 1)
         round_y(nc.vector.tensor_copy, last, 1, 1, 2)
         turn_y(last, 1, "h_bank", 3)

@@ -244,10 +244,10 @@ def tile_distilled_meson_correlator_k7_kernel(
         load_tau(0, 1)
         load_e(0)
         load_scale_rows(e_scales_first, snk_scales[0:2])
-        load_scale_rows(s_scales, src_scales)
         load_tau(1, 0)
-        load_s(0, 1)
         load_back(0)
+        load_s(0, 1)
+        load_scale_rows(s_scales, src_scales)
         load_tau(1, 1)
         load_scale_rows(e_scales_rest, snk_scales[2 : 2 * G])
         load_e(1)
@@ -297,7 +297,7 @@ def tile_distilled_meson_correlator_k7_kernel(
             ready = divmod(s + 3, 2)
             coming = divmod(s + 4, 2)
             scalar_is_free = coming[0] >= G
-            for n in range(3):
+            for n in (1, 0, 2):
                 stage2(s, n)
             if s >= 1:
                 round_y(gpsimd_copy, s - 1, 1, 0, 2, yt_il.get(s - 2))
@@ -306,14 +306,16 @@ def tile_distilled_meson_correlator_k7_kernel(
             weigh_h(s + 1, 0)
             stage1(s + 1, 3)
             weigh_y(s, 0)
+            stage2(s, 3)
             if s >= 1:
                 turn_y(s - 1, 0, "yt_bank", 2)
                 turn_y(s - 1, 1, "yt_bank", 2)
-            stage2(s, 3)
             weigh_y(s, 1)
-            if ready[0] < G:
+            if ready[0] < G and ready[1] == 1:
                 quantize_tau(*ready)
-            round_y(gpsimd_copy, s, 0, 0, 2, tau_il.get(ready))
+                round_y(gpsimd_copy, s, 0, 0, 2, tau_il[ready])
+            else:
+                round_y(gpsimd_copy, s, 0, 0, 2)
             weigh_h_on_scalar(s + 1, 3)
             weigh_h(s + 1, 1)
             weigh_y(s, 2)
@@ -321,7 +323,7 @@ def tile_distilled_meson_correlator_k7_kernel(
                 weigh_h(s + 1, 2)
             weigh_y(s, 3)
             if s + 2 < HALVES:
-                for k in range(3):
+                for k in (0, 2, 1) if scalar_is_free else (2, 1, 0):
                     stage1(s + 2, k)
             if s >= 1:
                 gather_yt(nc.scalar.copy, s - 1, 0)
@@ -330,36 +332,39 @@ def tile_distilled_meson_correlator_k7_kernel(
                 interleave_tau(nc.scalar.copy, coming[0], coming[1], 0, P)
             store_y(s, 0, 2)
             quantize_h(s + 1)
+            if ready[0] < G and ready[1] == 0:
+                quantize_tau(*ready)
             if s >= 1:
                 quantize_and_store_yt(s - 1, 0, KP)
 
-        for n in range(3):
-            stage2(last, n)
-        stage2(last, 3, "h_bank")
-        round_y(gpsimd_copy, last - 1, 1, 0, 2, yt_il[last - 2])
         turn_y(last - 1, 0, "yt_bank", 2)
-        turn_y(last - 1, 1, "yt_bank", 2)
+        gather_yt(nc.scalar.copy, last - 1, 0)
+        stage2(last, 1)
+        stage2(last, 0)
+        stage2(last, 3, "h_bank")
+        stage2(last, 2)
+        round_y(gpsimd_copy, last - 1, 1, 0, 2, yt_il[last - 2])
         weigh_y(last, 0)
         round_y(nc.scalar.copy, last, 0, 0, 1)
         weigh_y(last, 1)
         round_y(nc.scalar.copy, last, 0, 1, 2)
         store_y(last, 0, 1)
+        turn_y(last - 1, 1, "yt_bank", 2)
         turn_y(last, 0, "h_bank", 3)
-        gather_yt(nc.scalar.copy, last - 1, 0)
-        gather_yt(nc.scalar.copy, last - 1, 1)
         weigh_y(last, 2)
+        round_y(nc.scalar.copy, last, 1, 0, 1)
         weigh_y(last, 3)
         store_y(last, 1, 2)
-        round_y(nc.vector.tensor_copy, last, 1, 0, 1)
         round_y(nc.vector.tensor_copy, last, 1, 1, 2)
         turn_y(last, 1, "h_bank", 3)
-        quantize_and_store_yt(last - 1, 0, KP)
-        gather_yt(nc.scalar.copy, last, 0)
+        gather_yt(nc.scalar.copy, last - 1, 1)
+        gather_yt(nc.vector.tensor_copy, last, 0)
         gather_yt(nc.scalar.copy, last, 1)
+        quantize_and_store_yt(last - 1, 0, KP)
         quantize_and_store_yt(last, 0, KP // 2)
         quantize_and_store_yt(last, KP // 2, KP)
         for q in range(4):
-            nc.sync.dma_start(
+            nc.scalar.dma_start(
                 out=out_2[0, 4 * q : 4 * q + 4, :].rearrange("r (c m) -> c r m", c=G).bitcast(I32),
                 in_=y_scales[32 * q : 32 * q + 16, :].bitcast(I32),
             )

from contextlib import ExitStack

import concourse.mybir as mybir
from concourse.masks import make_identity

G, A, B = 4, 1024, 512
FLOPS = 2 * G * (A * A * B + A * B * B)

F32 = mybir.dt.float32
BF16 = mybir.dt.bfloat16
I32 = mybir.dt.int32
U32 = mybir.dt.uint32
U8 = mybir.dt.uint8
FP8X4 = mybir.dt.float8_e4m3fn_x4
FP4X4 = mybir.dt.float4_e2m1fn_x4
MULT = mybir.AluOpType.mult
ADD = mybir.AluOpType.add
COPY = mybir.ActivationFunctionType.Copy

P = 128
PACK = 4
KP = P * PACK
HALVES = 2 * G
SNK_ROWS = 2 * HALVES
SRC_ROW0 = 32
WROWS = SRC_ROW0 + G


def tile_distilled_meson_correlator_k7_kernel(
    tc, tau, back, src_weight, snk_weight, snk_words, snk_scales, src_words, src_scales, out_0, out_1, out_2
):
    nc = tc.nc
    with ExitStack() as ctx:
        keep = ctx.enter_context(tc.tile_pool(name="keep", bufs=1))
        work = ctx.enter_context(tc.tile_pool(name="work", bufs=2))
        psum = ctx.enter_context(tc.psum_pool(name="psum", bufs=1))
        ctx.enter_context(tc.manual_schedule())

        tau_raw, back_sb, e_words, s_words = {}, {}, {}, {}
        tau_il, tau_codes, tau_scales = {}, {}, {}
        h_bank, h_il, h_codes, h_scales = {}, {}, {}, {}
        chain_bank, y32, y16, yt_bank, yt_il = {}, {}, {}, {}, {}

        ident = keep.tile([P, P], F32, name="ident")
        w_rows16 = keep.tile([P, KP], BF16, name="w_rows16")
        w_rows32 = keep.tile([P, KP], F32, name="w_rows32")
        zero = keep.tile([P, 1], F32, name="zero")
        w_cols = keep.tile([P, WROWS, PACK], F32, name="w_cols")
        e_scales_first = keep.tile([P, 2, A], U8, name="e_scales_first", align_bytes=64)
        e_scales_rest = keep.tile([P, 2 * (G - 1), A], U8, name="e_scales_rest", align_bytes=64)
        s_scales = keep.tile([P, G, B], U8, name="s_scales", align_bytes=64)
        y_scales = keep.tile([P, A], U8, name="y_scales", align_bytes=64)

        def load_tau(c, g):
            tau_raw[c, g] = keep.tile([P, PACK, B], BF16, name="tau_raw_%d_%d" % (c, g))
            nc.sync.dma_start(
                out=tau_raw[c, g][:], in_=tau[c, g * KP : (g + 1) * KP, :].rearrange("(p j) b -> p j b", j=PACK)
            )

        def load_back(u):
            c, h = divmod(u, 2)
            back_sb[u] = keep.tile([P, PACK, B], BF16, name="back_%d" % u)
            nc.sync.dma_start(
                out=back_sb[u][:].rearrange("p (d e) j -> p d (e j)", e=2),
                in_=back[c, h * KP : (h + 1) * KP, :].rearrange("(d p e) j -> p d (e j)", d=2, e=2),
            )

        def load_e(c):
            e_words[c] = keep.tile([P, 2, 2 * A], U8, name="e_words_%d" % c, align_bytes=64)
            nc.sync.dma_start(
                out=e_words[c][:].bitcast(I32),
                in_=snk_words[2 * c : 2 * c + 2].rearrange("g p n -> p g n").bitcast(I32),
            )

        def load_s(c0, c1):
            words = keep.tile([P, c1 - c0, 2 * B], U8, name="s_words_%d" % c0, align_bytes=64)
            nc.sync.dma_start(
                out=words[:].bitcast(I32), in_=src_words[c0:c1].rearrange("g p n -> p g n").bitcast(I32)
            )
            for c in range(c0, c1):
                s_words[c] = words[:, c - c0, :]

        def load_scale_rows(plane, rows):
            for r in range(4):
                nc.sync.dma_start(
                    out=plane[r:P:32, :, :].bitcast(I32),
                    in_=rows[:, r:16:4, :].rearrange("g q n -> q g n").bitcast(I32),
                )

        def interleave_tau(copy, c, g, m0, m1):
            if (c, g) not in tau_il:
                tau_il[c, g] = work.tile([P, PACK * B], BF16, name="tau_il", bufs=3, align_bytes=64)
            dst = tau_il[c, g][:].rearrange("p (t a b j) -> p a t b j", t=PACK, b=2, j=PACK)
            src = tau_raw[c, g][:].rearrange("p j (a b t) -> p a t b j", b=2, t=PACK)
            copy(out=dst[:, m0 // 2 : m1 // 2], in_=src[:, m0 // 2 : m1 // 2])

        def quantize_tau(c, g):
            tau_codes[c, g] = work.tile([P, B], U32, name="tau_codes", bufs=4, align_bytes=64)
            tau_scales[c, g] = work.tile([P, B], U8, name="tau_scales", bufs=4, align_bytes=64)
            nc.vector.quantize_mx(
                out=tau_codes[c, g][:].bitcast(FP8X4), scales=tau_scales[c, g][:], in_=tau_il[c, g][:]
            )

        def stage1(u, k):
            c, h = divmod(u, 2)
            bank = psum.tile([P, PACK, P], F32, name="h_bank", bufs=3)
            h_bank[u, k] = bank
            i0 = h * KP + k * P
            for t in range(PACK):
                for g in range(2):
                    plane = e_scales_first[:, g, :] if c == 0 else e_scales_rest[:, 2 * (c - 1) + g, :]
                    nc.tensor.matmul_mx(
                        out=bank[:, t, :],
                        lhsT=tau_codes[c, g][:, t * P : (t + 1) * P].bitcast(FP8X4),
                        lhsT_scale=tau_scales[c, g][:, t * P : (t + 1) * P],
                        rhs=e_words[c][:, g, 2 * i0 : 2 * (i0 + P)].bitcast(FP4X4),
                        rhs_scale=plane[:, i0 : i0 + P],
                        start=(g == 0),
                        stop=(g == 1),
                    )

        def h_window(u, k):
            if u not in h_il:
                h_il[u] = work.tile([P, PACK, P, PACK], BF16, name="h_il", align_bytes=64)
            d, r0 = k // 2, 64 * (k % 2)
            return h_il[u][:, 2 * d : 2 * d + 2, r0 : r0 + 64, :]

        def weigh_h_on_scalar(u, k):
            row = SRC_ROW0 + u // 2
            slots = work.tile([P, PACK, 2, 64], BF16, name="h_slots")
            for t in range(PACK):
                nc.scalar.activation(
                    out=slots[:, t, :, :],
                    in_=h_bank[u, k][:, t, :].rearrange("p (r e) -> p e r", e=2),
                    func=COPY,
                    scale=w_cols[:, row, t : t + 1],
                )
            nc.scalar.copy(
                out=h_window(u, k).rearrange("p e (a b) t -> p e a t b", b=4),
                in_=slots[:].rearrange("p t e (a b) -> p e a t b", b=4),
            )

        def weigh_h(u, k):
            row = SRC_ROW0 + u // 2
            nc.vector.tensor_tensor(
                out=h_window(u, k).rearrange("p e r t -> p r e t"),
                in0=h_bank[u, k][:].rearrange("p t (r e) -> p r e t", e=2),
                in1=w_cols[:, row : row + 1, :].unsqueeze(1).broadcast_to([P, 64, 2, PACK]),
                op=MULT,
            )

        def quantize_h(u):
            h_codes[u] = work.tile([P, KP], U32, name="h_codes", align_bytes=64)
            h_scales[u] = work.tile([P, KP], U8, name="h_scales", align_bytes=64)
            nc.vector.quantize_mx(
                out=h_codes[u][:].bitcast(FP8X4),
                scales=h_scales[u][:],
                in_=h_il[u][:].rearrange("p n r t -> p (n r t)"),
            )

        def stage2(u, n, tag="chain_bank"):
            c = u // 2
            bank = psum.tile([P, B], F32, name=tag, bufs=3)
            chain_bank[u, n] = bank
            nc.tensor.matmul_mx(
                out=bank[:],
                lhsT=h_codes[u][:, n * P : (n + 1) * P].bitcast(FP8X4),
                lhsT_scale=h_scales[u][:, n * P : (n + 1) * P],
                rhs=s_words[c].bitcast(FP4X4),
                rhs_scale=s_scales[:, c, :],
                start=True,
                stop=True,
            )

        def weigh_y(u, n):
            if n == 0:
                y32[u] = work.tile([P, PACK, B], F32, name="y32", bufs=5)
            nc.vector.scalar_tensor_tensor(
                out=y32[u][:, n, :],
                in0=chain_bank[u, n][:],
                scalar=w_cols[:, 2 * u + n // 2, n % 2 : n % 2 + 1],
                in1=back_sb[u][:, n, :],
                op0=MULT,
                op1=MULT,
            )

        def gpsimd_copy(out, in_):
            nc.gpsimd.tensor_scalar(out=out, in0=in_, scalar1=1.0, scalar2=-0.0, op0=MULT, op1=ADD)

        def round_y(copy, u, pair, d0, d1, host=None):
            if (u, pair) not in y16:
                if host is None:
                    host = work.tile([P, 2 * B], BF16, name="y16", bufs=3)
                y16[u, pair] = host[:, 0 : 2 * B]
            dst = y16[u, pair].rearrange("p (e d m z) -> p e d m z", e=2, d=2, z=2)
            src = y32[u][:, 2 * pair : 2 * pair + 2, :].rearrange("p d (m e z) -> p e d m z", e=2, z=2)
            copy(out=dst[:, :, d0:d1], in_=src[:, :, d0:d1])

        def turn_y(u, pair, tag, bufs):
            bank = psum.tile([P, 2, 2, P], F32, name=tag, bufs=bufs)
            yt_bank[u, pair] = bank
            words = y16[u, pair].bitcast(F32)
            for d in range(2):
                for e in range(2):
                    x0 = (2 * e + d) * P
                    nc.tensor.transpose(bank[:, d, e, :], words[:, x0 : x0 + P], ident[:])

        def gather_yt(copy, u, pair):
            if pair == 0:
                yt_il[u] = work.tile([P, PACK * KP], BF16, name="yt_il", align_bytes=64)
            dst = yt_il[u][:].bitcast(F32).rearrange("p (d a b x) -> p d a x b", d=2, b=2, x=PACK)
            copy(out=dst[:, pair], in_=yt_bank[u, pair][:].rearrange("p d e (a b) -> p a (d e) b", b=2))

        def quantize_and_store_yt(u, m0, m1):
            c, h = divmod(u, 2)
            codes = work.tile([P, KP], U32, name="y_codes", bufs=5, align_bytes=64)
            nc.vector.quantize_mx(
                out=codes[:, m0:m1].bitcast(FP8X4),
                scales=y_scales[4 * c : P, h * KP + m0 : h * KP + m1],
                in_=yt_il[u][:, PACK * m0 : PACK * m1],
            )
            nc.sync.dma_start(
                out=out_1[0, :, u * KP + m0 : u * KP + m1, :].rearrange("p m t -> p (m t)").bitcast(I32),
                in_=codes[:, m0:m1].bitcast(I32),
            )

        def store_y(u, d0, d1):
            c, h = divmod(u, 2)
            rows = out_0[c, h * KP : (h + 1) * KP, :].rearrange("(d p e) j -> p d (e j)", d=2, e=2)
            nc.sync.dma_start(
                out=rows[:, d0:d1, :], in_=y32[u][:].rearrange("p (d e) j -> p d (e j)", e=2)[:, d0:d1, :]
            )

        nc.vector.memset(zero[:], 0.0)
        nc.vector.memset(e_scales_first[:].bitcast(I32), 0)
        nc.vector.memset(s_scales[:].bitcast(I32), 0)
        nc.vector.memset(e_scales_rest[:].bitcast(I32), 0)
        make_identity(nc, ident[:])

        nc.sync.dma_start(out=w_rows16[0:SNK_ROWS, 0 : 2 * P], in_=snk_weight.rearrange("c (n x) -> (c n) x", x=2 * P))
        nc.sync.dma_start(out=w_rows16[SRC_ROW0:WROWS, :], in_=src_weight)
        nc.scalar.copy(out=w_rows32[:], in_=zero[:].to_broadcast([P, KP]))
        load_tau(0, 0)
        load_tau(0, 1)
        load_e(0)
        load_scale_rows(e_scales_first, snk_scales[0:2])
        load_tau(1, 0)
        load_back(0)
        load_s(0, 1)
        load_scale_rows(s_scales, src_scales)
        load_tau(1, 1)
        load_scale_rows(e_scales_rest, snk_scales[2 : 2 * G])
        load_e(1)
        load_tau(2, 0)
        load_back(1)
        load_tau(2, 1)
        load_s(1, G)
        load_back(2)
        load_e(2)
        load_back(3)
        load_tau(3, 0)
        load_tau(3, 1)
        load_back(4)
        load_e(3)
        for u in range(5, HALVES):
            load_back(u)

        nc.vector.tensor_copy(out=w_rows32[SRC_ROW0:WROWS, :], in_=w_rows16[SRC_ROW0:WROWS, :])
        nc.vector.tensor_copy(
            out=w_rows32[0:SNK_ROWS, :].rearrange("p (x t) -> p x t", t=PACK)[:, :, 0:2],
            in_=w_rows16[0:SNK_ROWS, 0 : 2 * P].rearrange("p (x e) -> p x e", e=2),
        )
        w_bank = psum.tile([P, 2, 2, P], F32, name="yt_bank", bufs=2)
        w_bank_cols = w_bank[:].rearrange("p d e r -> p (d e) r")
        for t in range(PACK):
            nc.tensor.transpose(w_bank_cols[:, t, :], w_rows32[:, t:KP:PACK], ident[:])

        interleave_tau(nc.vector.tensor_copy, 0, 0, 0, 96)
        interleave_tau(nc.scalar.copy, 0, 0, 96, P)
        nc.scalar.copy(out=w_cols[:], in_=w_bank_cols[:, :, 0:WROWS].rearrange("p t r -> p r t"))
        interleave_tau(nc.vector.tensor_copy, 0, 1, 0, 64)
        interleave_tau(nc.scalar.copy, 0, 1, 64, P)
        quantize_tau(0, 0)
        quantize_tau(0, 1)
        for k in range(3):
            stage1(0, k)
        interleave_tau(nc.scalar.copy, 1, 0, 0, P)
        for k in range(PACK):
            weigh_h(0, k)
            stage1(*divmod(k + 3, PACK))
        quantize_h(0)
        quantize_tau(1, 0)
        interleave_tau(nc.scalar.copy, 1, 1, 0, P)

        last = HALVES - 1
        for s in range(last):
            ready = divmod(s + 3, 2)
            coming = divmod(s + 4, 2)
            scalar_is_free = coming[0] >= G
            for n in (1, 0, 2):
                stage2(s, n)
            if s >= 1:
                round_y(gpsimd_copy, s - 1, 1, 0, 2, yt_il.get(s - 2))
            if scalar_is_free:
                weigh_h_on_scalar(s + 1, 2)
            weigh_h(s + 1, 0)
            stage1(s + 1, 3)
            weigh_y(s, 0)
            stage2(s, 3)
            if s >= 1:
                turn_y(s - 1, 0, "yt_bank", 2)
                turn_y(s - 1, 1, "yt_bank", 2)
            weigh_y(s, 1)
            if ready[0] < G and ready[1] == 1:
                quantize_tau(*ready)
                round_y(gpsimd_copy, s, 0, 0, 2, tau_il[ready])
            else:
                round_y(gpsimd_copy, s, 0, 0, 2)
            weigh_h_on_scalar(s + 1, 3)
            weigh_h(s + 1, 1)
            weigh_y(s, 2)
            if not scalar_is_free:
                weigh_h(s + 1, 2)
            weigh_y(s, 3)
            if s + 2 < HALVES:
                for k in (0, 2, 1) if scalar_is_free else (2, 1, 0):
                    stage1(s + 2, k)
            if s >= 1:
                gather_yt(nc.scalar.copy, s - 1, 0)
                gather_yt(nc.scalar.copy, s - 1, 1)
            if coming[0] < G:
                interleave_tau(nc.scalar.copy, coming[0], coming[1], 0, P)
            store_y(s, 0, 2)
            quantize_h(s + 1)
            if ready[0] < G and ready[1] == 0:
                quantize_tau(*ready)
            if s >= 1:
                quantize_and_store_yt(s - 1, 0, KP)

        turn_y(last - 1, 0, "yt_bank", 2)
        gather_yt(nc.scalar.copy, last - 1, 0)
        stage2(last, 1)
        stage2(last, 0)
        stage2(last, 3, "h_bank")
        stage2(last, 2)
        round_y(gpsimd_copy, last - 1, 1, 0, 2, yt_il[last - 2])
        weigh_y(last, 0)
        round_y(nc.scalar.copy, last, 0, 0, 1)
        weigh_y(last, 1)
        round_y(nc.scalar.copy, last, 0, 1, 2)
        store_y(last, 0, 1)
        turn_y(last - 1, 1, "yt_bank", 2)
        turn_y(last, 0, "h_bank", 3)
        weigh_y(last, 2)
        round_y(nc.scalar.copy, last, 1, 0, 1)
        weigh_y(last, 3)
        store_y(last, 1, 2)
        round_y(nc.vector.tensor_copy, last, 1, 1, 2)
        turn_y(last, 1, "h_bank", 3)
        gather_yt(nc.scalar.copy, last - 1, 1)
        gather_yt(nc.vector.tensor_copy, last, 0)
        gather_yt(nc.scalar.copy, last, 1)
        quantize_and_store_yt(last - 1, 0, KP)
        quantize_and_store_yt(last, 0, KP // 2)
        quantize_and_store_yt(last, KP // 2, KP)
        for q in range(4):
            nc.scalar.dma_start(
                out=out_2[0, 4 * q : 4 * q + 4, :].rearrange("r (c m) -> c r m", c=G).bitcast(I32),
                in_=y_scales[32 * q : 32 * q + 16, :].bitcast(I32),
            )
